import numpy as np, ml_dtypes
CORES = [48,51,52,55]
N = 4
import mx_ref
BF = ml_dtypes.bfloat16
def entries(a):
    return np.ascontiguousarray(a.T).reshape(-1)
def table(e):
    return np.ascontiguousarray(np.reshape(e, (-1, 16)).T).astype(np.int32)
def cols(t, e):
    v = np.concatenate([t.reshape(128, -1, 4), np.zeros((128, 1, 4), BF)], axis=1)
    return np.ascontiguousarray(v[:, e]).reshape(128, -1)
def decode(q):
    o = []
    for b in range(4):
        e = np.zeros((128, 128, 4), np.float32); e[np.arange(128), np.arange(128), b] = 1
        o.append(mx_ref.matmul(mx_ref.quantize(e.reshape(128, 512).astype(BF)), q))
    return np.stack(o, axis=2).reshape(128, -1)
def f(rng, *shape):
    return mx_ref.flush((rng.standard_normal(shape, dtype=np.float32) * np.exp2(rng.integers(-2, 3, shape[:-1] + (1,)))).astype(BF))
def wide(rng, *shape, cols=0):
    v = rng.standard_normal(shape, dtype=np.float32) * np.exp2(rng.integers(-12, 13, shape)).astype(np.float32)
    if cols: v *= np.repeat(np.exp2(rng.integers(-cols, cols + 1, shape[:-2] + (1, shape[-1] // 4))) * (rng.random(shape[:-2] + (1, shape[-1] // 4)) > 0.0625), 4, axis=-1).astype(np.float32)
    return mx_ref.flush(v.astype(BF))
TC, T, CAPP, O = 1024, 256, 96, 1
def lists(rng, n, front=False):
    a = np.full((N, N, CAPP), -1)
    b = np.full((N, N, CAPP), -1)
    for s in range(N):
        for d in range(N):
            k = rng.permutation(CAPP)[:n[s, d]]
            a[s, d, k] = rng.integers(0, T, len(k)); b[d, s, k] = 0
    for d in range(N):
        used = b[d] == 0; u = int(used.sum())
        b[d][used] = np.arange(u) if front else rng.permutation(TC)[:u]
    return {"snd": np.stack([table(a[s]) for s in range(N)]), "plc": np.stack([table(b[d]) for d in range(N)])}
def tiles(rng):
    return {"kc": f(rng, N, 128, 4 * TC), "x": f(rng, N, 128, 4 * T), "qw": f(rng, N, 128, 512 * O)}
def setup_inputs(rng):
    return {**tiles(rng), **lists(rng, rng.integers(0, CAPP + 1, (N, N)))}
def setup_inputs_full(rng):
    return {**tiles(rng), **lists(rng, np.full((N, N), CAPP))}
def setup_inputs_few(rng):
    n = rng.integers(0, 3, (N, N))
    for d in range(N):
        o = rng.permutation([s for s in range(N) if s != d])
        n[o[0], d] = 0; n[o[1], d] = 1
    n[:, rng.integers(0, N)] = 0
    return {**tiles(rng), **lists(rng, n)}
def setup_inputs_front(rng):
    return {**tiles(rng), **lists(rng, rng.integers(1, CAPP + 1, (N, N)), front=True)}
def setup_inputs_own(rng):
    n = rng.integers(0, 3, (N, N)); n[np.arange(N), np.arange(N)] = CAPP
    return {**tiles(rng), **lists(rng, n)}
def setup_inputs_spread(rng):
    d = setup_inputs(rng); d["x"] = wide(rng, N, 128, 4 * T, cols=8); d["kc"] = wide(rng, N, 128, 4 * TC); return d
def check_inputs(d):
    b = []
    a = np.stack([entries(d["snd"][r]).reshape(N, CAPP) for r in range(N)])
    p = np.stack([entries(d["plc"][r]).reshape(N, CAPP) for r in range(N)])
    if a.min() < -1 or a.max() >= T: b.append("snd")
    if p.min() < -1 or p.max() >= TC: b.append("plc")
    if ((a.transpose(1, 0, 2) == -1) != (p == -1)).any(): b.append("plc is -1 exactly where the slot is empty")
    for r in range(N):
        v = p[r][p[r] != -1].tolist()
        if len(set(v)) != len(v): b.append("plc differs"); break
    return b
def reference(kc, x, qw, snd, plc):
    y = np.zeros((N, 128, O * TC), np.float32)
    for r in range(N):
        sent = np.concatenate([cols(x[s], entries(snd[s])[r * CAPP:(r + 1) * CAPP]) for s in range(N)], axis=1)
        got = decode(mx_ref.quantize(sent)).astype(BF).reshape(128, N * CAPP, 4)
        p = entries(plc[r]); used = p >= 0
        c = kc[r].reshape(128, TC, 4).copy()
        c[:, p[used]] = got[:, used]
        c = mx_ref.quantize(np.ascontiguousarray(c).reshape(128, 4 * TC))
        for o in range(O):
            y[r][:, TC * o:TC * o + TC] = mx_ref.matmul(mx_ref.quantize(np.ascontiguousarray(qw[r][:, 512 * o:512 * o + 512])), c)
    return {"y": y}

@@ -1,0 +1,279 @@
+from concourse.bass import DstId, RemoteDMATransfer
+from concourse.mybir import dt, AluOpType, ActivationFunctionType
+
+TC, TX, CAPP, N = 1024, 256, 96, 4
+LC = CAPP // 16
+WW = 1232
+SRC = TC + N * CAPP
+BF, F32, I32, U16, U8, C8 = "bfloat16", "float32", "int32", "uint16", "uint8", "float8_e4m3fn_x4"
+
+SCRATCH = {
+    "sl": ("sbuf", [128, N * LC], I32),
+    "offs": ("sbuf", [128, 4 * N * LC], U16),
+    "xs": ("sbuf", [128, 4 * TX], BF),
+    "kcs": ("sbuf", [128, 4 * TC], BF),
+    "qws": ("sbuf", [128, 512], BF),
+    "h1": ("sbuf", [128, 4 * 192], BF),
+    "h2": ("sbuf", [128, 4 * 192], BF),
+    "sq": ("sbuf", [128, 192], C8), "ss": ("sbuf", [128, 192], U8),
+    "lq": ("sbuf", [128, 192], C8), "ls": ("sbuf", [128, 192], U8),
+    "cq": ("sbuf", [128, 288], C8), "cs": ("sbuf", [128, 288], U8),
+    "ones": ("sbuf", [128, 128], BF),
+    "ed": ("sbuf", [128, 516], BF),
+    "eq": ("sbuf", [128, 512], C8), "es": ("sbuf", [128, 512], U8),
+    "wq": ("sbuf", [128, 128], C8), "ws": ("sbuf", [128, 128], U8),
+    "kq": ("sbuf", [128, TC], C8), "ks": ("sbuf", [128, TC], U8),
+    "dO": ("sbuf", [128, 512], BF), "dX": ("sbuf", [128, 768], BF), "dP": ("sbuf", [128, 512], BF),
+    "oq": ("sbuf", [128, 128], C8), "osc": ("sbuf", [128, 128], U8),
+    "fq": ("sbuf", [128, 192], C8), "fs": ("sbuf", [128, 192], U8),
+    "pq": ("sbuf", [128, 128], C8), "psc": ("sbuf", [128, 128], U8),
+    "zt": ("sbuf", [128, WW // 2], BF),
+    "win": ("sbuf", [128, WW], F32),
+    "vals": ("sbuf", [128, CAPP], F32),
+    "dump": ("sbuf", [128, LC], I32),
+    "pl": ("sbuf", [128, LC], I32), "pu1": ("sbuf", [128, LC], I32), "pv": ("sbuf", [128, LC], I32),
+    "pn": ("sbuf", [128, LC], I32), "pw": ("sbuf", [128, LC], I32), "pm": ("sbuf", [128, LC], I32),
+    "pp": ("sbuf", [128, LC], I32), "pf": ("sbuf", [128, LC], I32), "offp": ("sbuf", [128, LC], U16),
+    "ia": ("sbuf", [32, 64], I32), "ib": ("sbuf", [32, 64], I32), "ic": ("sbuf", [32, 64], I32),
+    "ident": ("sbuf", [32, 64], F32),
+    "off4": ("sbuf", [32, 256], F32), "mx1": ("sbuf", [32, 128], F32), "mx2": ("sbuf", [32, 64], F32),
+    "mx3": ("sbuf", [32, 64], F32),
+    "offy": ("sbuf", [128, 64], U16),
+    "yb": ("sbuf", [128, SRC], F32),
+    "yo": ("sbuf", [128, TC], F32),
+    "pun": ("psum", [128, 2048], F32),
+    "pro": ("psum", [128, 2048], F32),
+}
+SEMAPHORES = ["vec", "act", "ten", "gps", "ldl", "ldx", "ldp", "ldw", "ldk0", "ldk1", "inv", "ax", "ap", "sent", "st0", "st1"]
+
+
+def rank_program(g, core, T, topo):
+    rank = T.rank_of(core)
+    if rank is None:
+        return
+    A, COPY = AluOpType, ActivationFunctionType.Copy
+    Q = {"vec": g.vector, "act": g.scalar, "ten": g.tensor, "gps": g, "syn": g.sync}
+    n = {"vec": 0, "act": 0, "ten": 0, "gps": 0}
+    seen = {}
+
+    def did(q, call):
+        n[q] += 1
+        call.then_inc(T.sem[q], 1)
+        return n[q]
+
+    def need(q, key, val):
+        if seen.get((q, key), 0) < val:
+            Q[q].wait_ge(T.sem[key], val)
+            seen[(q, key)] = val
+
+    die = [topo.die(c) for c in T.cores]
+    near = [r for r in range(N) if die[r] == die[rank]]
+    far = [r for r in range(N) if die[r] != die[rank]]
+    pos = near.index(rank)
+    mate = near[1 - pos]
+
+    def dst(r):
+        rid, pid, _ = topo.addr(T.cores[r])
+        return DstId(rid=rid, pnc=pid)
+
+    def mask(r, k, step):
+        return sum(1 << e for e in topo.engines(core, T.cores[r])[k::step])
+
+    g.sync.dma_start(T.sl[0:16, :], T.snd[:]).then_inc(T.sem.ldl, 16)
+    g.scalar.dma_start(T.sl[16:32, :], T.snd[:]).then_inc(T.sem.ldl, 16)
+    g.sync.dma_start(T.xs[0:64, :], T.x[0:64, :]).then_inc(T.sem.ldx, 16)
+    g.scalar.dma_start(T.xs[64:128, :], T.x[64:128, :]).then_inc(T.sem.ldx, 16)
+    for h in range(N):
+        g.sync.dma_start(T.pl[16 * h:16 * h + 16, :], T.plc[:, LC * h:LC * h + LC]).then_inc(T.sem.ldp, 16)
+    g.scalar.dma_start(T.qws[:], T.qw[:]).then_inc(T.sem.ldw, 16)
+    for k in range(2):
+        g.sync.dma_start(T.kcs[:, 2048 * k:2048 * k + 2048], T.kc[:, 2048 * k:2048 * k + 2048]).then_inc(T.sem["ldk%d" % k], 16)
+
+    did("vec", g.vector.memset(T.ones[:], 1.0))
+    v_ed = did("vec", g.vector.memset(T.ed[:], 0.0))
+    v_zt = did("vec", g.vector.memset(T.zt[:], 0.0))
+    need("gps", "vec", v_ed)
+    p_ed = did("gps", g.affine_select(T.ed[:, 4:516:4], T.ones[:], [[-1, 128]], A.is_equal, 0.0, 0, 1))
+    did("gps", g.iota(T.ia[:], [[0, 64]], 0, 1))
+    p_ib = did("gps", g.iota(T.ib[:], [[16, 64]], 0, 0))
+    did("gps", g.iota(T.dump[:], [[16, LC]], TC, 1))
+    p_all = did("gps", g.iota(T.vals[:], [[1, CAPP]], TC, CAPP // 16, allow_small_or_imprecise_dtypes=True))
+    need("act", "vec", v_zt)
+    for k in range(2):
+        a_win = did("act", g.scalar.activation(T.win[:, WW // 2 * k:WW // 2 * (k + 1)], T.zt[:], COPY))
+    need("vec", "gps", p_ed)
+    for b in range(4):
+        v_eq = did("vec", g.vector.quantize_mx(T.eq[:, 128 * b:128 * b + 128], T.es[:, 128 * b:128 * b + 128], T.ed[:, 4 - b:516 - b]))
+    need("vec", "gps", p_ib)
+    v = did("vec", g.vector.tensor_scalar(T.ic[:], T.ia[:], 15, None, A.bitwise_and))
+    need("vec", "vec", v)
+    v_id = did("vec", g.vector.tensor_tensor(T.ident[:], T.ic[:], T.ib[:], A.add))
+
+    need("vec", "ldl", 32)
+    for q in (32, 64, 96):
+        v = did("vec", g.vector.tensor_copy(T.sl[q:q + 32, :], T.sl[0:32, :]))
+    need("vec", "vec", v)
+    for t in (2, 0, 3, 1):
+        v_of = did("vec", g.vector.tensor_scalar(T.offs[:, 24 * t:24 * t + 24], T.sl[:], 4.0, float(t), A.mult, A.add))
+
+    def gather(buf, lo):
+        def win(t):
+            return T.xs[:, 0:4 * TX].indirect(T.offs[:, 24 * t + LC * lo:24 * t + LC * lo + 2 * LC])
+        for q in ("vec", "act"):
+            need(q, "vec", v_of)
+            need(q, "ldx", 32)
+        for t in (0, 1):
+            vv = did("vec", g.vector.tensor_copy(T[buf][:, t:768:4], win(t)))
+            aa = did("act", g.scalar.activation(T[buf][:, t + 2:768:4], win(t + 2), COPY))
+        return vv, aa
+
+    vv, aa = gather("h1", far[0])
+    need("vec", "vec", vv)
+    need("vec", "act", aa)
+    v_q1 = did("vec", g.vector.quantize_mx(T.sq[:], T.ss[:], T.h1[:]))
+    need("gps", "vec", v_q1)
+    land = slice(CAPP * pos, CAPP * pos + CAPP)
+    for codes in (True, False):
+        tr = []
+        for k in range(2):
+            here = slice(CAPP * k, CAPP * k + CAPP)
+            if codes:
+                a, b = T.sq[:, here].bitcast(dt.uint8), T.lq[:, land].bitcast(dt.uint8)
+            else:
+                a, b = T.ss[:, here], T.ls[:, land]
+            tr.append(RemoteDMATransfer(dst_ids=[dst(far[k])], dma_engine_mask=mask(far[k], k, 2), remote_sem=T.sem.ax, src=a, dst=b))
+        g.remote_dma_fused(tr, local_sem=T.sem.sent)
+
+    c0 = CAPP * (1 - pos)
+    sent, come = (slice(192, 288), slice(0, 96)) if pos == 0 else (slice(0, 96), slice(192, 288))
+    vv, aa = gather("h2", near[0])
+    need("vec", "vec", vv)
+    need("vec", "act", aa)
+    v_q2 = did("vec", g.vector.quantize_mx(T.cq[:, c0:c0 + 192], T.cs[:, c0:c0 + 192], T.h2[:]))
+    need("gps", "vec", v_q2)
+    rid, pid, _ = topo.addr(T.cores[mate])
+    g.remote_dma(T.cq[:, sent].bitcast(dt.uint8), T.cq[:, sent].bitcast(dt.uint8), T.sem.ap, T.sem.sent, pid, rid, mask(mate, 0, 1))
+    g.remote_dma(T.cs[:, sent], T.cs[:, sent], T.sem.ap, T.sem.sent, pid, rid, mask(mate, 0, 1))
+
+    def unpack(codes, scales, w, after):
+        out = []
+        for b in range(4):
+            if after:
+                need("ten", after[b][0], after[b][1])
+            out.append(did("ten", g.tensor.matmul_mx(T.pun[:, 512 * b:512 * b + w], T.eq[:, 128 * b:128 * b + 128], T.es[:, 128 * b:128 * b + 128],
+                                                     codes, scales, True, True)))
+        return out
+
+    def cast(q, buf, w, b, t):
+        need(q, "ten", t)
+        o, i = T[buf][:, b:4 * w:4], T.pun[:, 512 * b:512 * b + w]
+        return (q, did(q, g.vector.tensor_copy(o, i) if q == "vec" else g.scalar.activation(o, i, COPY)))
+
+    own0 = 96 if pos == 0 else 64
+    need("ten", "vec", v_q2)
+    tO = unpack(T.cq[:, own0:own0 + 128], T.cs[:, own0:own0 + 128], 128, None)
+    cO = [cast("act", "dO", 128, b, tO[b]) for b in range(4)]
+
+    need("vec", "ldp", 64)
+    need("vec", "gps", p_all)
+    v = did("vec", g.vector.tensor_copy(T.pl[64:128, :], T.pl[0:64, :]))
+    need("vec", "vec", v)
+    did("vec", g.vector.tensor_scalar(T.pu1[:], T.pl[:], 15, None, A.bitwise_and))
+    did("vec", g.vector.tensor_scalar(T.pn[:], T.pl[:], 0.0, None, A.is_lt))
+    v = did("vec", g.vector.tensor_scalar(T.pv[:], T.pl[:], 4, None, A.arith_shift_right))
+    need("vec", "vec", v)
+    did("vec", g.vector.tensor_scalar(T.pw[:], T.pu1[:], 64.0, None, A.mult))
+    v = did("vec", g.vector.tensor_tensor(T.pm[:], T.pn[:], T.dump[:], A.mult))
+    need("vec", "vec", v)
+    v = did("vec", g.vector.tensor_tensor(T.pp[:], T.pw[:], T.pv[:], A.add))
+    need("vec", "vec", v)
+    v = did("vec", g.vector.tensor_tensor(T.pf[:], T.pp[:], T.pm[:], A.max))
+    need("vec", "vec", v)
+    v = did("vec", g.vector.tensor_copy(T.offp[:], T.pf[:]))
+    need("vec", "vec", v)
+    need("vec", "act", a_win)
+    v_in = did("vec", g.vector.tensor_copy(T.win[:, 0:WW].indirect(T.offp[:, 0:LC]), T.vals[:]))
+    need("syn", "vec", v_in)
+    for h in range(N):
+        for q in range(2):
+            g.sync.dma_start(T.off4[16 * q:16 * q + 16, 64 * h:64 * h + 64], T.win[16 * h:16 * h + 1, 0:TC]).then_inc(T.sem.inv, 16)
+
+    def times(bank, w, codes, scales):
+        return did("ten", g.tensor.matmul_mx(T.pro[:, 512 * bank:512 * bank + w], T.wq[:], T.ws[:], codes, scales, True, True))
+
+    need("vec", "ldw", 16)
+    did("vec", g.vector.quantize_mx(T.wq[:], T.ws[:], T.qws[:]))
+    need("vec", "act", cO[3][1])
+    v_oq = did("vec", g.vector.quantize_mx(T.oq[:], T.osc[:], T.dO[:]))
+    v_k = []
+    for k in range(2):
+        need("vec", "ldk%d" % k, 16)
+        v_k.append(did("vec", g.vector.quantize_mx(T.kq[:, 512 * k:512 * k + 512], T.ks[:, 512 * k:512 * k + 512], T.kcs[:, 2048 * k:2048 * k + 2048])))
+    need("ten", "vec", v_oq)
+    t_o = times(2, 128, T.oq[:], T.osc[:])
+    t_k = []
+    for k in range(2):
+        need("ten", "vec", v_k[k])
+        t_k.append(times(k, 512, T.kq[:, 512 * k:512 * k + 512], T.ks[:, 512 * k:512 * k + 512]))
+
+    def take(r, cnt, bank, col, t):
+        need("act", "ten", t)
+        c = TC + CAPP * r
+        return did("act", g.scalar.activation(T.yb[:, c:c + cnt], T.pro[:, 512 * bank + col:512 * bank + col + cnt], COPY))
+
+    take(rank, CAPP, 2, 32 * pos, t_o)
+    for k in range(2):
+        need("act", "ten", t_k[k])
+        a_k = did("act", g.scalar.activation(T.yb[:, 512 * k:512 * k + 512], T.pro[:, 512 * k:512 * k + 512], COPY))
+
+    ENG = {0: "vec", 1: "act", 2: "vec", 3: "act"}
+    need("ten", "ax", 32)
+    tX = unpack(T.lq[:], T.ls[:], 192, cO)
+    cX = [cast(ENG[b], "dX", 192, b, tX[b]) for b in range(4)]
+    need("ten", "ap", 32)
+    p0 = 0 if pos == 0 else 160
+    tP = unpack(T.cq[:, p0:p0 + 128], T.cs[:, p0:p0 + 128], 128, cX)
+    need("vec", "vec", cX[2][1])
+    need("vec", "act", cX[3][1])
+    v_x = did("vec", g.vector.quantize_mx(T.fq[:], T.fs[:], T.dX[:]))
+    cP = [cast(ENG[b], "dP", 128, b, tP[b]) for b in range(4)]
+    need("ten", "vec", v_x)
+    t_x = times(3, 192, T.fq[:], T.fs[:])
+    need("vec", "vec", cP[2][1])
+    need("vec", "act", cP[3][1])
+    v_p = did("vec", g.vector.quantize_mx(T.pq[:], T.psc[:], T.dP[:]))
+    need("ten", "vec", v_p)
+    need("ten", "act", a_k)
+    t_p = times(0, 128, T.pq[:], T.psc[:])
+    take(far[0], 2 * CAPP, 3, 0, t_x)
+    a_y = take(mate, CAPP, 0, 32 * pos, t_p)
+
+    need("vec", "inv", 128)
+    v = did("vec", g.vector.tensor_tensor(T.mx1[:], T.off4[:, 0:128], T.off4[:, 128:256], A.max))
+    need("vec", "vec", v)
+    v = did("vec", g.vector.tensor_tensor(T.mx2[:], T.mx1[:, 0:64], T.mx1[:, 64:128], A.max))
+    need("vec", "vec", v)
+    v = did("vec", g.vector.tensor_tensor(T.mx3[:], T.mx2[:], T.ident[:], A.max))
+    need("vec", "vec", v)
+    for q in (0, 32, 64, 96):
+        v_oy = did("vec", g.vector.tensor_copy(T.offy[q:q + 32, :], T.mx3[:]))
+
+    for q in ("vec", "act"):
+        need(q, "vec", v_oy)
+        need(q, "act", a_y)
+    cut = (0, 14, 28, 46, 64)
+    for k in range(2):
+        for q, c in (("vec", 2 * k), ("act", 2 * k + 1)):
+            lo, hi = cut[c], cut[c + 1]
+            o, i = T.yo[:, 16 * lo:16 * hi], T.yb[:, 0:SRC].indirect(T.offy[:, lo:hi])
+            did(q, g.vector.tensor_copy(o, i) if q == "vec" else g.scalar.activation(o, i, COPY))
+        need("syn", "vec", n["vec"])
+        need("syn", "act", n["act"])
+        lo, hi = 16 * cut[2 * k], 16 * cut[2 * k + 2]
+        g.sync.dma_start(T.y[:, lo:hi], T.yo[:, lo:hi]).then_inc(T.sem["st%d" % k], 16)
+
+    need("gps", "sent", 64)
+    for q in ("vec", "act", "ten", "gps"):
+        need("gps", q, n[q])
+    for k in range(2):
+        g.sync.wait_ge(T.sem["st%d" % k], 16)

@@ -8,25 +8,26 @@ SRC = TC + N * CAPP
 BF, F32, I32, U16, U8, C8 = "bfloat16", "float32", "int32", "uint16", "uint8", "float8_e4m3fn_x4"
 
 SCRATCH = {
-    "sl": ("sbuf", [128, N * LC], I32),
-    "offs": ("sbuf", [128, 4 * N * LC], U16),
+    "sl": ("sbuf", [32, N * LC], I32),
+    "offs": ("sbuf", [128, N * LC], U16),
+    "off4": ("sbuf", [128, 4 * 8], U16),
     "xs": ("sbuf", [128, 4 * TX], BF),
     "kcs": ("sbuf", [128, 4 * TC], BF),
     "qws": ("sbuf", [128, 512], BF),
-    "h1": ("sbuf", [128, 4 * 192], BF),
-    "h2": ("sbuf", [128, 4 * 192], BF),
+    "xq": ("sbuf", [128, TX], C8), "xsc": ("sbuf", [128, TX], U8),
+    "db": ("sbuf", [128, 4 * TX], BF),
+    "hn": ("sbuf", [128, 512], BF), "hf": ("sbuf", [128, 768], BF), "ho": ("sbuf", [128, 512], BF),
+    "cq": ("sbuf", [128, 224], C8), "cs": ("sbuf", [128, 224], U8),
     "sq": ("sbuf", [128, 192], C8), "ss": ("sbuf", [128, 192], U8),
     "lq": ("sbuf", [128, 192], C8), "ls": ("sbuf", [128, 192], U8),
-    "cq": ("sbuf", [128, 288], C8), "cs": ("sbuf", [128, 288], U8),
+    "oq": ("sbuf", [128, 128], C8), "osc": ("sbuf", [128, 128], U8),
+    "dn": ("sbuf", [128, 512], BF),
+    "nq": ("sbuf", [128, 128], C8), "nsc": ("sbuf", [128, 128], U8),
     "ones": ("sbuf", [128, 128], BF),
     "ed": ("sbuf", [128, 516], BF),
     "eq": ("sbuf", [128, 512], C8), "es": ("sbuf", [128, 512], U8),
     "wq": ("sbuf", [128, 128], C8), "ws": ("sbuf", [128, 128], U8),
     "kq": ("sbuf", [128, TC], C8), "ks": ("sbuf", [128, TC], U8),
-    "dO": ("sbuf", [128, 512], BF), "dX": ("sbuf", [128, 768], BF), "dP": ("sbuf", [128, 512], BF),
-    "oq": ("sbuf", [128, 128], C8), "osc": ("sbuf", [128, 128], U8),
-    "fq": ("sbuf", [128, 192], C8), "fs": ("sbuf", [128, 192], U8),
-    "pq": ("sbuf", [128, 128], C8), "psc": ("sbuf", [128, 128], U8),
     "zt": ("sbuf", [128, WW // 2], BF),
     "win": ("sbuf", [128, WW], F32),
     "vals": ("sbuf", [128, CAPP], F32),
@@ -36,7 +37,7 @@ SCRATCH = {
     "pp": ("sbuf", [128, LC], I32), "pf": ("sbuf", [128, LC], I32), "offp": ("sbuf", [128, LC], U16),
     "ia": ("sbuf", [32, 64], I32), "ib": ("sbuf", [32, 64], I32), "ic": ("sbuf", [32, 64], I32),
     "ident": ("sbuf", [32, 64], F32),
-    "off4": ("sbuf", [32, 256], F32), "mx1": ("sbuf", [32, 128], F32), "mx2": ("sbuf", [32, 64], F32),
+    "inv4": ("sbuf", [32, 256], F32), "mx1": ("sbuf", [32, 128], F32), "mx2": ("sbuf", [32, 64], F32),
     "mx3": ("sbuf", [32, 64], F32),
     "offy": ("sbuf", [128, 64], U16),
     "yb": ("sbuf", [128, SRC], F32),
@@ -44,7 +45,7 @@ SCRATCH = {
     "pun": ("psum", [128, 2048], F32),
     "pro": ("psum", [128, 2048], F32),
 }
-SEMAPHORES = ["vec", "act", "ten", "gps", "ldl", "ldx", "ldp", "ldw", "ldk0", "ldk1", "inv", "ax", "ap", "sent", "st0", "st1"]
+SEMAPHORES = ["vec", "act", "ten", "gps", "ldl", "ldx0", "ldx1", "ldp", "ldw", "ldk0", "ldk1", "inv", "af", "an", "sent", "st0", "st1"]
 
 
 def rank_program(g, core, T, topo):
@@ -66,6 +67,18 @@ def rank_program(g, core, T, topo):
             Q[q].wait_ge(T.sem[key], val)
             seen[(q, key)] = val
 
+    def copy(q, o, i):
+        return did(q, g.vector.tensor_copy(o, i) if q == "vec" else g.scalar.activation(o, i, COPY))
+
+    def quant(codes, scales, tile):
+        return did("vec", g.vector.quantize_mx(codes, scales, tile))
+
+    def tt(o, a, b, op):
+        return did("vec", g.vector.tensor_tensor(T[o][:], a, b, op))
+
+    def ts(o, a, c, op):
+        return did("vec", g.vector.tensor_scalar(T[o][:], T[a][:], c, None, op))
+
     die = [topo.die(c) for c in T.cores]
     near = [r for r in range(N) if die[r] == die[rank]]
     far = [r for r in range(N) if die[r] != die[rank]]
@@ -81,10 +94,11 @@ def rank_program(g, core, T, topo):
 
     g.sync.dma_start(T.sl[0:16, :], T.snd[:]).then_inc(T.sem.ldl, 16)
     g.scalar.dma_start(T.sl[16:32, :], T.snd[:]).then_inc(T.sem.ldl, 16)
-    g.sync.dma_start(T.xs[0:64, :], T.x[0:64, :]).then_inc(T.sem.ldx, 16)
-    g.scalar.dma_start(T.xs[64:128, :], T.x[64:128, :]).then_inc(T.sem.ldx, 16)
     for h in range(N):
-        g.sync.dma_start(T.pl[16 * h:16 * h + 16, :], T.plc[:, LC * h:LC * h + LC]).then_inc(T.sem.ldp, 16)
+        q = g.sync if h % 2 else g.scalar
+        q.dma_start(T.pl[16 * h:16 * h + 16, :], T.plc[:, LC * h:LC * h + LC]).then_inc(T.sem.ldp, 16)
+    g.sync.dma_start(T.xs[:, 0:512], T.x[:, 0:512]).then_inc(T.sem.ldx0, 16)
+    g.scalar.dma_start(T.xs[:, 512:1024], T.x[:, 512:1024]).then_inc(T.sem.ldx1, 16)
     g.scalar.dma_start(T.qws[:], T.qw[:]).then_inc(T.sem.ldw, 16)
     for k in range(2):
         g.sync.dma_start(T.kcs[:, 2048 * k:2048 * k + 2048], T.kc[:, 2048 * k:2048 * k + 2048]).then_inc(T.sem["ldk%d" % k], 16)
@@ -100,38 +114,112 @@ def rank_program(g, core, T, topo):
     p_all = did("gps", g.iota(T.vals[:], [[1, CAPP]], TC, CAPP // 16, allow_small_or_imprecise_dtypes=True))
     need("act", "vec", v_zt)
     for k in range(2):
-        a_win = did("act", g.scalar.activation(T.win[:, WW // 2 * k:WW // 2 * (k + 1)], T.zt[:], COPY))
+        a_win = copy("act", T.win[:, WW // 2 * k:WW // 2 * (k + 1)], T.zt[:])
     need("vec", "gps", p_ed)
     for b in range(4):
-        v_eq = did("vec", g.vector.quantize_mx(T.eq[:, 128 * b:128 * b + 128], T.es[:, 128 * b:128 * b + 128], T.ed[:, 4 - b:516 - b]))
+        v_eq = quant(T.eq[:, 128 * b:128 * b + 128], T.es[:, 128 * b:128 * b + 128], T.ed[:, 4 - b:516 - b])
     need("vec", "gps", p_ib)
-    v = did("vec", g.vector.tensor_scalar(T.ic[:], T.ia[:], 15, None, A.bitwise_and))
+    v = ts("ic", "ia", 15, A.bitwise_and)
     need("vec", "vec", v)
-    v_id = did("vec", g.vector.tensor_tensor(T.ident[:], T.ic[:], T.ib[:], A.add))
+    v_id = tt("ident", T.ic[:], T.ib[:], A.add)
 
     need("vec", "ldl", 32)
-    for q in (32, 64, 96):
-        v = did("vec", g.vector.tensor_copy(T.sl[q:q + 32, :], T.sl[0:32, :]))
-    need("vec", "vec", v)
-    for t in (2, 0, 3, 1):
-        v_of = did("vec", g.vector.tensor_scalar(T.offs[:, 24 * t:24 * t + 24], T.sl[:], 4.0, float(t), A.mult, A.add))
+    for q in (0, 32, 64, 96):
+        v_of = did("vec", g.vector.tensor_copy(T.offs[q:q + 32, :], T.sl[:]))
+    need("vec", "ldp", 64)
+    v_pl = did("vec", g.vector.tensor_copy(T.pl[64:128, :], T.pl[0:64, :]))
+    c_near = LC * near[0] + (4 if pos == 0 else 0)
+    c_own = LC * near[0] + (0 if pos == 0 else 4)
+    need("vec", "vec", v_of)
+    for t in range(4):
+        v_o4 = did("vec", g.vector.tensor_scalar(T.off4[:, 8 * t:8 * t + 8], T.offs[:, c_near:c_near + 8], 4.0, float(t), A.mult, A.add))
 
-    def gather(buf, lo):
-        def win(t):
-            return T.xs[:, 0:4 * TX].indirect(T.offs[:, 24 * t + LC * lo:24 * t + LC * lo + 2 * LC])
-        for q in ("vec", "act"):
-            need(q, "vec", v_of)
-            need(q, "ldx", 32)
-        for t in (0, 1):
-            vv = did("vec", g.vector.tensor_copy(T[buf][:, t:768:4], win(t)))
-            aa = did("act", g.scalar.activation(T[buf][:, t + 2:768:4], win(t + 2), COPY))
-        return vv, aa
+    ENG = ("vec", "act", "vec", "act")
+    v_xq = []
 
-    vv, aa = gather("h1", far[0])
+    def quant_x(k):
+        need("vec", "ldx%d" % k, 16)
+        v_xq.append(quant(T.xq[:, 128 * k:128 * k + 128], T.xsc[:, 128 * k:128 * k + 128], T.xs[:, 512 * k:512 * k + 512]))
+
+    def unpack(b, codes, scales, lo):
+        c = 128 * b
+        return did("ten", g.tensor.matmul_mx(T.pun[:, 512 * b:512 * b + 128], T.eq[:, c:c + 128], T.es[:, c:c + 128],
+                                             T[codes][:, lo:lo + 128], T[scales][:, lo:lo + 128], True, True))
+
+    def unpack_x(k, b, after):
+        need("ten", "vec", max(v_eq, v_xq[k]))
+        if after:
+            need("ten", ENG[b], after)
+        return unpack(b, "xq", "xsc", 128 * k)
+
+    def cast(k, b, t):
+        need(ENG[b], "ten", t)
+        c = TX * b + 128 * k
+        return copy(ENG[b], T.db[:, c:c + 128], T.pun[:, 512 * b:512 * b + 128])
+
+    def gather_near(q, t):
+        need(q, "vec", v_o4)
+        need(q, "ldx0", 16)
+        need(q, "ldx1", 16)
+        return copy(q, T.hn[:, t:512:4], T.xs[:, 0:4 * TX].indirect(T.off4[:, 8 * t:8 * t + 8]))
+
+    def gather(q, buf, c, k, t):
+        need(q, ENG[t], cx[t])
+        return copy(q, T[buf][:, t:64 * k:4], T.db[:, TX * t:TX * t + TX].indirect(T.offs[:, c:c + k]))
+
+    quant_x(0)
+    tx = [unpack_x(0, b, None) for b in range(4)]
+    need("vec", "vec", v_pl)
+    ts("pu1", "pl", 15, A.bitwise_and)
+    ts("pn", "pl", 0.0, A.is_lt)
+    v_pl = ts("pv", "pl", 4, A.arith_shift_right)
+    c0 = [cast(0, b, tx[b]) for b in (0, 1)]
+    quant_x(1)
+
+    gather_near("vec", 0)
+    gather_near("act", 1)
+    vv = gather_near("vec", 2)
+    aa = gather_near("act", 3)
     need("vec", "vec", vv)
     need("vec", "act", aa)
-    v_q1 = did("vec", g.vector.quantize_mx(T.sq[:], T.ss[:], T.h1[:]))
-    need("gps", "vec", v_q1)
+    q0 = 96 * (1 - pos)
+    v_qn = quant(T.cq[:, q0:q0 + 128], T.cs[:, q0:q0 + 128], T.hn[:])
+    need("gps", "vec", v_qn)
+    rid, pid, _ = topo.addr(T.cores[mate])
+    sent = slice(128, 224) if pos == 0 else slice(0, 96)
+    g.remote_dma(T.cq[:, sent].bitcast(dt.uint8), T.cq[:, sent].bitcast(dt.uint8), T.sem.an, T.sem.sent, pid, rid, mask(mate, 0, 1))
+    g.remote_dma(T.cs[:, sent], T.cs[:, sent], T.sem.an, T.sem.sent, pid, rid, mask(mate, 0, 1))
+
+    need("vec", "vec", v_pl)
+    need("vec", "gps", p_all)
+    v_pw = ts("pw", "pu1", 64.0, A.mult)
+    v_pm = tt("pm", T.pn[:], T.dump[:], A.mult)
+    c0 += [cast(0, b, tx[b]) for b in (2, 3)]
+    need("vec", "vec", v_pm)
+    v_pp = tt("pp", T.pw[:], T.pv[:], A.add)
+    tx = [unpack_x(1, b, c0[b]) for b in range(4)]
+    cx = [cast(1, b, tx[b]) for b in (0, 1)]
+    c_far = LC * far[0]
+    need("vec", "vec", v_pp)
+    v_pf = tt("pf", T.pp[:], T.pm[:], A.max)
+    vv = gather("vec", "hf", c_far, 12, 0)
+    gather("act", "hf", c_far, 12, 1)
+    cx += [cast(1, b, tx[b]) for b in (2, 3)]
+    need("vec", "vec", v_pf)
+    v_op = did("vec", g.vector.tensor_copy(T.offp[:], T.pf[:]))
+    need("vec", "vec", v_op)
+    need("vec", "act", a_win)
+    v_in = did("vec", g.vector.tensor_copy(T.win[:, 0:WW].indirect(T.offp[:, 0:LC]), T.vals[:]))
+    need("syn", "vec", v_in)
+    for h in range(N):
+        for q in range(2):
+            g.sync.dma_start(T.inv4[16 * q:16 * q + 16, 64 * h:64 * h + 64], T.win[16 * h:16 * h + 1, 0:TC]).then_inc(T.sem.inv, 16)
+    gather("act", "hf", c_far, 12, 3)
+    aa = gather("act", "hf", c_far, 12, 2)
+    need("vec", "vec", vv)
+    need("vec", "act", aa)
+    v_qf = quant(T.sq[:], T.ss[:], T.hf[:])
+    need("gps", "vec", v_qf)
     land = slice(CAPP * pos, CAPP * pos + CAPP)
     for codes in (True, False):
         tr = []
@@ -141,132 +229,89 @@ def rank_program(g, core, T, topo):
                 a, b = T.sq[:, here].bitcast(dt.uint8), T.lq[:, land].bitcast(dt.uint8)
             else:
                 a, b = T.ss[:, here], T.ls[:, land]
-            tr.append(RemoteDMATransfer(dst_ids=[dst(far[k])], dma_engine_mask=mask(far[k], k, 2), remote_sem=T.sem.ax, src=a, dst=b))
+            tr.append(RemoteDMATransfer(dst_ids=[dst(far[k])], dma_engine_mask=mask(far[k], k, 2), remote_sem=T.sem.af, src=a, dst=b))
         g.remote_dma_fused(tr, local_sem=T.sem.sent)
 
-    c0 = CAPP * (1 - pos)
-    sent, come = (slice(192, 288), slice(0, 96)) if pos == 0 else (slice(0, 96), slice(192, 288))
-    vv, aa = gather("h2", near[0])
-    need("vec", "vec", vv)
-    need("vec", "act", aa)
-    v_q2 = did("vec", g.vector.quantize_mx(T.cq[:, c0:c0 + 192], T.cs[:, c0:c0 + 192], T.h2[:]))
-    need("gps", "vec", v_q2)
-    rid, pid, _ = topo.addr(T.cores[mate])
-    g.remote_dma(T.cq[:, sent].bitcast(dt.uint8), T.cq[:, sent].bitcast(dt.uint8), T.sem.ap, T.sem.sent, pid, rid, mask(mate, 0, 1))
-    g.remote_dma(T.cs[:, sent], T.cs[:, sent], T.sem.ap, T.sem.sent, pid, rid, mask(mate, 0, 1))
+    def times(bank, codes, scales, a, b):
+        return did("ten", g.tensor.matmul_mx(T.pro[:, 512 * bank:512 * bank + b - a], T.wq[:], T.ws[:], T[codes][:, a:b], T[scales][:, a:b], True, True))
 
-    def unpack(codes, scales, w, after):
-        out = []
-        for b in range(4):
-            if after:
-                need("ten", after[b][0], after[b][1])
-            out.append(did("ten", g.tensor.matmul_mx(T.pun[:, 512 * b:512 * b + w], T.eq[:, 128 * b:128 * b + 128], T.es[:, 128 * b:128 * b + 128],
-                                                     codes, scales, True, True)))
-        return out
+    KC = ((0, 512, 0, "act"), (512, 768, 1, "act"), (768, 1024, 3, "vec"))
 
-    def cast(q, buf, w, b, t):
+    def quant_kc(k):
+        a, b = KC[k][:2]
+        need("vec", "ldk%d" % (a // 512), 16)
+        return quant(T.kq[:, a:b], T.ks[:, a:b], T.kcs[:, 4 * a:4 * b])
+
+    def times_kc(k, v):
+        a, b, bank, q = KC[k]
+        need("ten", "vec", v)
+        return times(bank, "kq", "ks", a, b)
+
+    def take_kc(k, t):
+        a, b, bank, q = KC[k]
         need(q, "ten", t)
-        o, i = T[buf][:, b:4 * w:4], T.pun[:, 512 * b:512 * b + w]
-        return (q, did(q, g.vector.tensor_copy(o, i) if q == "vec" else g.scalar.activation(o, i, COPY)))
-
-    own0 = 96 if pos == 0 else 64
-    need("ten", "vec", v_q2)
-    tO = unpack(T.cq[:, own0:own0 + 128], T.cs[:, own0:own0 + 128], 128, None)
-    cO = [cast("act", "dO", 128, b, tO[b]) for b in range(4)]
-
-    need("vec", "ldp", 64)
-    need("vec", "gps", p_all)
-    v = did("vec", g.vector.tensor_copy(T.pl[64:128, :], T.pl[0:64, :]))
-    need("vec", "vec", v)
-    did("vec", g.vector.tensor_scalar(T.pu1[:], T.pl[:], 15, None, A.bitwise_and))
-    did("vec", g.vector.tensor_scalar(T.pn[:], T.pl[:], 0.0, None, A.is_lt))
-    v = did("vec", g.vector.tensor_scalar(T.pv[:], T.pl[:], 4, None, A.arith_shift_right))
-    need("vec", "vec", v)
-    did("vec", g.vector.tensor_scalar(T.pw[:], T.pu1[:], 64.0, None, A.mult))
-    v = did("vec", g.vector.tensor_tensor(T.pm[:], T.pn[:], T.dump[:], A.mult))
-    need("vec", "vec", v)
-    v = did("vec", g.vector.tensor_tensor(T.pp[:], T.pw[:], T.pv[:], A.add))
-    need("vec", "vec", v)
-    v = did("vec", g.vector.tensor_tensor(T.pf[:], T.pp[:], T.pm[:], A.max))
-    need("vec", "vec", v)
-    v = did("vec", g.vector.tensor_copy(T.offp[:], T.pf[:]))
-    need("vec", "vec", v)
-    need("vec", "act", a_win)
-    v_in = did("vec", g.vector.tensor_copy(T.win[:, 0:WW].indirect(T.offp[:, 0:LC]), T.vals[:]))
-    need("syn", "vec", v_in)
-    for h in range(N):
-        for q in range(2):
-            g.sync.dma_start(T.off4[16 * q:16 * q + 16, 64 * h:64 * h + 64], T.win[16 * h:16 * h + 1, 0:TC]).then_inc(T.sem.inv, 16)
-
-    def times(bank, w, codes, scales):
-        return did("ten", g.tensor.matmul_mx(T.pro[:, 512 * bank:512 * bank + w], T.wq[:], T.ws[:], codes, scales, True, True))
-
-    need("vec", "ldw", 16)
-    did("vec", g.vector.quantize_mx(T.wq[:], T.ws[:], T.qws[:]))
-    need("vec", "act", cO[3][1])
-    v_oq = did("vec", g.vector.quantize_mx(T.oq[:], T.osc[:], T.dO[:]))
-    v_k = []
-    for k in range(2):
-        need("vec", "ldk%d" % k, 16)
-        v_k.append(did("vec", g.vector.quantize_mx(T.kq[:, 512 * k:512 * k + 512], T.ks[:, 512 * k:512 * k + 512], T.kcs[:, 2048 * k:2048 * k + 2048])))
-    need("ten", "vec", v_oq)
-    t_o = times(2, 128, T.oq[:], T.osc[:])
-    t_k = []
-    for k in range(2):
-        need("ten", "vec", v_k[k])
-        t_k.append(times(k, 512, T.kq[:, 512 * k:512 * k + 512], T.ks[:, 512 * k:512 * k + 512]))
+        return copy(q, T.yb[:, a:b], T.pro[:, 512 * bank:512 * bank + b - a])
 
     def take(r, cnt, bank, col, t):
         need("act", "ten", t)
         c = TC + CAPP * r
-        return did("act", g.scalar.activation(T.yb[:, c:c + cnt], T.pro[:, 512 * bank + col:512 * bank + col + cnt], COPY))
+        return copy("act", T.yb[:, c:c + cnt], T.pro[:, 512 * bank + col:512 * bank + col + cnt])
 
-    take(rank, CAPP, 2, 32 * pos, t_o)
-    for k in range(2):
-        need("act", "ten", t_k[k])
-        a_k = did("act", g.scalar.activation(T.yb[:, 512 * k:512 * k + 512], T.pro[:, 512 * k:512 * k + 512], COPY))
+    for t in range(4):
+        aa = gather("act", "ho", c_own, 8, t)
+    need("vec", "ldw", 16)
+    v_wq = quant(T.wq[:], T.ws[:], T.qws[:])
+    v_k = [quant_kc(0)]
+    need("vec", "act", aa)
+    v_oq = quant(T.oq[:], T.osc[:], T.ho[:])
+    v_k += [quant_kc(1), quant_kc(2)]
+    need("ten", "vec", v_wq)
+    t_k = [times_kc(0, v_k[0])]
+    need("ten", "vec", v_oq)
+    t_o = times(2, "oq", "osc", 0, 128)
+    a_k = take_kc(0, t_k[0])
+    a_o = take(rank, CAPP, 2, 32 * pos, t_o)
 
-    ENG = {0: "vec", 1: "act", 2: "vec", 3: "act"}
-    need("ten", "ax", 32)
-    tX = unpack(T.lq[:], T.ls[:], 192, cO)
-    cX = [cast(ENG[b], "dX", 192, b, tX[b]) for b in range(4)]
-    need("ten", "ap", 32)
-    p0 = 0 if pos == 0 else 160
-    tP = unpack(T.cq[:, p0:p0 + 128], T.cs[:, p0:p0 + 128], 128, cX)
-    need("vec", "vec", cX[2][1])
-    need("vec", "act", cX[3][1])
-    v_x = did("vec", g.vector.quantize_mx(T.fq[:], T.fs[:], T.dX[:]))
-    cP = [cast(ENG[b], "dP", 128, b, tP[b]) for b in range(4)]
-    need("ten", "vec", v_x)
-    t_x = times(3, 192, T.fq[:], T.fs[:])
-    need("vec", "vec", cP[2][1])
-    need("vec", "act", cP[3][1])
-    v_p = did("vec", g.vector.quantize_mx(T.pq[:], T.psc[:], T.dP[:]))
-    need("ten", "vec", v_p)
-    need("ten", "act", a_k)
-    t_p = times(0, 128, T.pq[:], T.psc[:])
-    take(far[0], 2 * CAPP, 3, 0, t_x)
-    a_y = take(mate, CAPP, 0, 32 * pos, t_p)
-
+    need("ten", "an", 32)
+    for b in range(4):
+        need("ten", ENG[b], cx[b])
+    p0 = 0 if pos == 0 else 96
+    tn = [unpack(b, "cq", "cs", p0) for b in range(4)]
+    for b in range(4):
+        need("act", "ten", tn[b])
+        aa = copy("act", T.dn[:, b:512:4], T.pun[:, 512 * b:512 * b + 128])
+    t_k += [times_kc(1, v_k[1]), times_kc(2, v_k[2])]
+    take_kc(1, t_k[1])
     need("vec", "inv", 128)
-    v = did("vec", g.vector.tensor_tensor(T.mx1[:], T.off4[:, 0:128], T.off4[:, 128:256], A.max))
+    v = tt("mx1", T.inv4[:, 0:128], T.inv4[:, 128:256], A.max)
     need("vec", "vec", v)
-    v = did("vec", g.vector.tensor_tensor(T.mx2[:], T.mx1[:, 0:64], T.mx1[:, 64:128], A.max))
+    v = tt("mx2", T.mx1[:, 0:64], T.mx1[:, 64:128], A.max)
+    need("vec", "act", aa)
+    v_nq = quant(T.nq[:], T.nsc[:], T.dn[:])
     need("vec", "vec", v)
-    v = did("vec", g.vector.tensor_tensor(T.mx3[:], T.mx2[:], T.ident[:], A.max))
+    v = tt("mx3", T.mx2[:], T.ident[:], A.max)
+    take_kc(2, t_k[2])
     need("vec", "vec", v)
     for q in (0, 32, 64, 96):
         v_oy = did("vec", g.vector.tensor_copy(T.offy[q:q + 32, :], T.mx3[:]))
+    need("ten", "vec", v_nq)
+    need("ten", "act", a_o)
+    t_n = times(2, "nq", "nsc", 0, 128)
+    take(mate, CAPP, 2, 32 * pos, t_n)
+
+    need("ten", "af", 32)
+    need("ten", "act", a_k)
+    t_f = times(0, "lq", "ls", 0, 192)
+    a_y = take(far[0], 2 * CAPP, 0, 0, t_f)
 
     for q in ("vec", "act"):
         need(q, "vec", v_oy)
         need(q, "act", a_y)
-    cut = (0, 14, 28, 46, 64)
+    cut = (0, 12, 24, 44, 64)
     for k in range(2):
         for q, c in (("vec", 2 * k), ("act", 2 * k + 1)):
             lo, hi = cut[c], cut[c + 1]
-            o, i = T.yo[:, 16 * lo:16 * hi], T.yb[:, 0:SRC].indirect(T.offy[:, lo:hi])
-            did(q, g.vector.tensor_copy(o, i) if q == "vec" else g.scalar.activation(o, i, COPY))
+            copy(q, T.yo[:, 16 * lo:16 * hi], T.yb[:, 0:SRC].indirect(T.offy[:, lo:hi]))
         need("syn", "vec", n["vec"])
         need("syn", "act", n["act"])
         lo, hi = 16 * cut[2 * k], 16 * cut[2 * k + 2]

@@ -8,76 +8,63 @@ SRC = TC + N * CAPP
 BF, F32, I32, U16, U8, C8 = "bfloat16", "float32", "int32", "uint16", "uint8", "float8_e4m3fn_x4"
 
 SCRATCH = {
-    "sl": ("sbuf", [32, N * LC], I32),
+    "sl": ("sbuf", [64, N * LC], I32),
     "offs": ("sbuf", [128, N * LC], U16),
-    "off4": ("sbuf", [128, 4 * 8], U16),
+    "off4": ("sbuf", [128, 4 * LC], U16),
     "xs": ("sbuf", [128, 4 * TX], BF),
     "kcs": ("sbuf", [128, 4 * TC], BF),
     "qws": ("sbuf", [128, 512], BF),
     "xq": ("sbuf", [128, TX], C8), "xsc": ("sbuf", [128, TX], U8),
     "db": ("sbuf", [128, 4 * TX], BF),
     "hn": ("sbuf", [128, 512], BF), "hf": ("sbuf", [128, 768], BF), "ho": ("sbuf", [128, 512], BF),
-    "cq": ("sbuf", [128, 224], C8), "cs": ("sbuf", [128, 224], U8),
-    "sq": ("sbuf", [128, 192], C8), "ss": ("sbuf", [128, 192], U8),
+    "nq": ("sbuf", [128, 224], C8), "ns": ("sbuf", [128, 224], U8),
+    "fq": ("sbuf", [128, 192], C8), "fs": ("sbuf", [128, 192], U8),
     "lq": ("sbuf", [128, 192], C8), "ls": ("sbuf", [128, 192], U8),
     "oq": ("sbuf", [128, 128], C8), "osc": ("sbuf", [128, 128], U8),
     "dn": ("sbuf", [128, 512], BF),
-    "nq": ("sbuf", [128, 128], C8), "nsc": ("sbuf", [128, 128], U8),
+    "dq": ("sbuf", [128, 128], C8), "dsc": ("sbuf", [128, 128], U8),
     "ones": ("sbuf", [128, 128], BF),
     "ed": ("sbuf", [128, 516], BF),
     "eq": ("sbuf", [128, 512], C8), "es": ("sbuf", [128, 512], U8),
     "wq": ("sbuf", [128, 128], C8), "ws": ("sbuf", [128, 128], U8),
     "kq": ("sbuf", [128, TC], C8), "ks": ("sbuf", [128, TC], U8),
-    "zt": ("sbuf", [128, WW // 2], BF),
     "win": ("sbuf", [128, WW], F32),
     "vals": ("sbuf", [128, CAPP], F32),
     "dump": ("sbuf", [128, LC], I32),
-    "pl": ("sbuf", [128, LC], I32), "pu1": ("sbuf", [128, LC], I32), "pv": ("sbuf", [128, LC], I32),
-    "pn": ("sbuf", [128, LC], I32), "pw": ("sbuf", [128, LC], I32), "pm": ("sbuf", [128, LC], I32),
-    "pp": ("sbuf", [128, LC], I32), "pf": ("sbuf", [128, LC], I32), "offp": ("sbuf", [128, LC], U16),
-    "ia": ("sbuf", [32, 64], I32), "ib": ("sbuf", [32, 64], I32), "ic": ("sbuf", [32, 64], I32),
-    "ident": ("sbuf", [32, 64], F32),
+    "pl": ("sbuf", [128, LC], I32), "pu": ("sbuf", [128, LC], I32), "pv": ("sbuf", [128, LC], I32),
+    "pw": ("sbuf", [128, LC], I32), "pp": ("sbuf", [128, LC], I32), "pf": ("sbuf", [128, LC], I32),
+    "offp": ("sbuf", [128, LC], U16),
+    "pa": ("sbuf", [32, 1], F32), "pc": ("sbuf", [32, 1], F32),
     "inv4": ("sbuf", [32, 256], F32), "mx1": ("sbuf", [32, 128], F32), "mx2": ("sbuf", [32, 64], F32),
-    "mx3": ("sbuf", [32, 64], F32),
     "offy": ("sbuf", [128, 64], U16),
     "yb": ("sbuf", [128, SRC], F32),
     "yo": ("sbuf", [128, TC], F32),
     "pun": ("psum", [128, 2048], F32),
     "pro": ("psum", [128, 2048], F32),
 }
-SEMAPHORES = ["vec", "act", "ten", "gps", "ldl", "ldx0", "ldx1", "ldp", "ldw", "ldk0", "ldk1", "inv", "af", "an", "sent", "st0", "st1"]
+SEMAPHORES = ["ldl", "ldx0", "ldx1", "ldp", "ldw", "ldk0", "ldk1", "vec", "act", "ten", "gps", "inv", "af", "an", "sent",
+              "st0", "st1", "st2"]
+CUT = (0, 8, 16, 28, 40, 52, 64)
+PIECES = len(CUT) // 2
+KC = ((0, 512), (512, 768), (768, 1024))
+ORDER = {
+    "gps": "win0 aff dump pl vals sn pa sf pc",
+    "act": "win2 win4 win8 zn gn3 gn1 gn0 cast1 gf1 cast2 cast3 gf3 zd zo go2 go1 go0 go3 ck0 dc1 dc3 dc0 co ck1 ck2 cn "
+           "ya0 ya1 ya2",
+    "vec": "ed ones eq0 eq3 of0 eq1 of1 pv o42 o43 o41 o40 xq1 xq0 gn2 pu eq2 pw qn pp cast0 pf wq op gf0 sc gf2 qf "
+           "kq0 kq2 oq kq1 mx1 mx2 oy3 oy1 dc2 oy0 dq oy2 cf yv0 yv1 yv2",
+    "ten": "u1 u0 u2 u3 k0 o r3 r1 r2 r0 k1 k2 f n",
+    "syn": "inv st0 st1 st2",
+}
 
 
 def rank_program(g, core, T, topo):
     rank = T.rank_of(core)
     if rank is None:
         return
-    A, COPY = AluOpType, ActivationFunctionType.Copy
-    Q = {"vec": g.vector, "act": g.scalar, "ten": g.tensor, "gps": g, "syn": g.sync}
-    n = {"vec": 0, "act": 0, "ten": 0, "gps": 0}
-    seen = {}
-
-    def did(q, call):
-        n[q] += 1
-        call.then_inc(T.sem[q], 1)
-        return n[q]
-
-    def need(q, key, val):
-        if seen.get((q, key), 0) < val:
-            Q[q].wait_ge(T.sem[key], val)
-            seen[(q, key)] = val
-
-    def copy(q, o, i):
-        return did(q, g.vector.tensor_copy(o, i) if q == "vec" else g.scalar.activation(o, i, COPY))
-
-    def quant(codes, scales, tile):
-        return did("vec", g.vector.quantize_mx(codes, scales, tile))
-
-    def tt(o, a, b, op):
-        return did("vec", g.vector.tensor_tensor(T[o][:], a, b, op))
-
-    def ts(o, a, c, op):
-        return did("vec", g.vector.tensor_scalar(T[o][:], T[a][:], c, None, op))
+    A, COPY, IDENT = AluOpType, ActivationFunctionType.Copy, ActivationFunctionType.Identity
+    V, S = g.vector, g.scalar
+    Q = {"vec": V, "act": S, "ten": g.tensor, "gps": g, "syn": g.sync}
 
     die = [topo.die(c) for c in T.cores]
     near = [r for r in range(N) if die[r] == die[rank]]
@@ -85,15 +72,12 @@ def rank_program(g, core, T, topo):
     pos = near.index(rank)
     mate = near[1 - pos]
 
-    def dst(r):
-        rid, pid, _ = topo.addr(T.cores[r])
-        return DstId(rid=rid, pnc=pid)
-
     def mask(r, k, step):
         return sum(1 << e for e in topo.engines(core, T.cores[r])[k::step])
 
-    g.sync.dma_start(T.sl[0:16, :], T.snd[:]).then_inc(T.sem.ldl, 16)
-    g.scalar.dma_start(T.sl[16:32, :], T.snd[:]).then_inc(T.sem.ldl, 16)
+    for h in range(4):
+        q = g.sync if h % 2 else g.scalar
+        q.dma_start(T.sl[16 * h:16 * h + 16, :], T.snd[:]).then_inc(T.sem.ldl, 16)
     for h in range(N):
         q = g.sync if h % 2 else g.scalar
         q.dma_start(T.pl[16 * h:16 * h + 16, :], T.plc[:, LC * h:LC * h + LC]).then_inc(T.sem.ldp, 16)
@@ -102,223 +86,170 @@ def rank_program(g, core, T, topo):
     g.scalar.dma_start(T.qws[:], T.qw[:]).then_inc(T.sem.ldw, 16)
     for k in range(2):
         g.sync.dma_start(T.kcs[:, 2048 * k:2048 * k + 2048], T.kc[:, 2048 * k:2048 * k + 2048]).then_inc(T.sem["ldk%d" % k], 16)
+    count = {"ldl": 64, "ldp": 64, "ldx0": 16, "ldx1": 16, "ldw": 16, "ldk0": 16, "ldk1": 16, "an": 32, "af": 32, "inv": 64}
 
-    did("vec", g.vector.memset(T.ones[:], 1.0))
-    v_ed = did("vec", g.vector.memset(T.ed[:], 0.0))
-    v_zt = did("vec", g.vector.memset(T.zt[:], 0.0))
-    need("gps", "vec", v_ed)
-    p_ed = did("gps", g.affine_select(T.ed[:, 4:516:4], T.ones[:], [[-1, 128]], A.is_equal, 0.0, 0, 1))
-    did("gps", g.iota(T.ia[:], [[0, 64]], 0, 1))
-    p_ib = did("gps", g.iota(T.ib[:], [[16, 64]], 0, 0))
-    did("gps", g.iota(T.dump[:], [[16, LC]], TC, 1))
-    p_all = did("gps", g.iota(T.vals[:], [[1, CAPP]], TC, CAPP // 16, allow_small_or_imprecise_dtypes=True))
-    need("act", "vec", v_zt)
+    ops = {}
+
+    def op(name, after, call):
+        ops[name] = (after.split(), call)
+
+    def quant(name, after, codes, scales, lo, hi, tile, start):
+        op(name, after, lambda q: V.quantize_mx(T[codes][:, lo:hi], T[scales][:, lo:hi], T[tile][:, start:start + 4 * (hi - lo)]))
+
+    def copy(name, after, out, in_):
+        op(name, after, lambda q: V.tensor_copy(out, in_) if q == "vec" else S.activation(out, in_, COPY))
+
+    def ts(name, after, o, a, c, f):
+        op(name, after, lambda q: V.tensor_scalar(T[o][:], T[a][:], c, None, f))
+
+    def tt(name, after, o, a, b, f):
+        op(name, after, lambda q: V.tensor_tensor(T[o][:], a, b, f))
+
+    op("ones", "", lambda q: V.memset(T.ones[:], 1.0))
+    op("ed", "", lambda q: V.memset(T.ed[:], 0.0))
+    op("aff", "ones ed", lambda q: g.affine_select(T.ed[:, 4:516:4], T.ones[:], [[-1, 128]], A.is_equal, 0.0, 0, 1))
+    for b in range(4):
+        quant("eq%d" % b, "aff", "eq", "es", 128 * b, 128 * b + 128, "ed", 4 - b)
+    zn = 384 * pos
+    for name, o in (("zn", T.hn[:, zn:zn + 128]), ("zo", T.ho[:, 384:512]), ("zd", T.dn[:, 384:512])):
+        op(name, "ones", lambda q, o=o: S.activation(o, T.ones[:], COPY, 0.0, 0.0))
+
+    imp = {"allow_small_or_imprecise_dtypes": True}
+    op("win0", "", lambda q: g.iota(T.win[:, 0:128], [[1, 2], [16, 64]], -3 * CAPP, LC, **imp))
+    for k, b in ((2, 0), (4, 2), (8, 4)):
+        op("win%d" % k, "win0 win%d" % b, lambda q, k=k: S.activation(T.win[:, 64 * k:128 * k], T.win[:, 0:64 * k], IDENT, float(k)))
+    op("dump", "", lambda q: g.iota(T.dump[:], [[16, LC]], TC, 1))
+    op("pl", "dump", lambda q: g.iota(T.pl[64:128, :], [[16, LC]], 0, 1))
+    op("vals", "pl", lambda q: g.iota(T.vals[:], [[1, CAPP]], TC, LC, **imp))
+    op("pa", "vals", lambda q: g.iota(T.pa[:], [[0, 1]], LC, 0, **imp))
+    op("pc", "pa", lambda q: g.affine_select(T.pc[:], T.pa[:], [[0, 1]], A.is_ge, 0.0, -16, 1))
+    ts("pu", "@ldp pl", "pu", "pl", 15, A.bitwise_and)
+    ts("pv", "@ldp pl", "pv", "pl", 4, A.logical_shift_right)
+    ts("pw", "pu", "pw", "pu", 64.0, A.mult)
+    tt("pp", "pw pv", "pp", T.pw[:], T.pv[:], A.add)
+    tt("pf", "pp dump", "pf", T.pp[:], T.dump[:], A.min)
+    copy("op", "pf", T.offp[:], T.pf[:])
+    copy("sc", "op vals win0 win8", T.win[:, 0:WW].indirect(T.offp[:, 0:LC]), T.vals[:])
+
+    def lay_out(q):
+        for h in range(N):
+            g.sync.dma_start(T.inv4[:, 64 * h:64 * h + 64], T.win[16 * h:16 * h + 2, 0:TC]).then_inc(T.sem.inv, 16)
+
+    op("inv", "sc", lay_out)
+    tt("mx1", "@inv", "mx1", T.inv4[:, 0:128], T.inv4[:, 128:256], A.max)
+    tt("mx2", "mx1", "mx2", T.mx1[:, 0:64], T.mx1[:, 64:128], A.max)
+    for k in range(4):
+        op("oy%d" % k, "mx2 pc", lambda q, k=k: V.tensor_scalar(T.offy[32 * k:32 * k + 32, :], T.mx2[:], T.pc[:], None, A.subtract))
+
     for k in range(2):
-        a_win = copy("act", T.win[:, WW // 2 * k:WW // 2 * (k + 1)], T.zt[:])
-    need("vec", "gps", p_ed)
+        copy("of%d" % k, "@ldl", T.offs[64 * k:64 * k + 64, :], T.sl[:])
+        quant("xq%d" % k, "@ldx%d" % k, "xq", "xsc", 128 * k, 128 * k + 128, "xs", 512 * k)
+    lo = 128 * (1 - pos)
     for b in range(4):
-        v_eq = quant(T.eq[:, 128 * b:128 * b + 128], T.es[:, 128 * b:128 * b + 128], T.ed[:, 4 - b:516 - b])
-    need("vec", "gps", p_ib)
-    v = ts("ic", "ia", 15, A.bitwise_and)
-    need("vec", "vec", v)
-    v_id = tt("ident", T.ic[:], T.ib[:], A.add)
+        op("o4%d" % b, "of0 of1", lambda q, b=b: V.tensor_scalar(T.off4[:, LC * b:LC * b + LC], T.offs[:, LC * mate:LC * mate + LC],
+                                                                 4.0, float(b), A.mult, A.add))
+        copy("gn%d" % b, "o4%d @ldx0 @ldx1" % b, T.hn[:, lo + b:lo + 384:4], T.xs[:, 0:4 * TX].indirect(T.off4[:, LC * b:LC * b + LC]))
+    tile = 96 * (1 - pos)
+    quant("qn", "zn gn0 gn1 gn2 gn3", "nq", "ns", tile, tile + 128, "hn", 0)
 
-    need("vec", "ldl", 32)
-    for q in (0, 32, 64, 96):
-        v_of = did("vec", g.vector.tensor_copy(T.offs[q:q + 32, :], T.sl[:]))
-    need("vec", "ldp", 64)
-    v_pl = did("vec", g.vector.tensor_copy(T.pl[64:128, :], T.pl[0:64, :]))
-    c_near = LC * near[0] + (4 if pos == 0 else 0)
-    c_own = LC * near[0] + (0 if pos == 0 else 4)
-    need("vec", "vec", v_of)
-    for t in range(4):
-        v_o4 = did("vec", g.vector.tensor_scalar(T.off4[:, 8 * t:8 * t + 8], T.offs[:, c_near:c_near + 8], 4.0, float(t), A.mult, A.add))
+    def send_near(q):
+        rid, pid, _ = topo.addr(T.cores[mate])
+        here = slice(128, 224) if pos == 0 else slice(0, 96)
+        g.remote_dma(T.nq[:, here].bitcast(dt.uint8), T.nq[:, here].bitcast(dt.uint8), T.sem.an, T.sem.sent, pid, rid, mask(mate, 0, 1))
+        g.remote_dma(T.ns[:, here], T.ns[:, here], T.sem.an, T.sem.sent, pid, rid, mask(mate, 0, 1))
 
-    ENG = ("vec", "act", "vec", "act")
-    v_xq = []
+    op("sn", "qn", send_near)
 
-    def quant_x(k):
-        need("vec", "ldx%d" % k, 16)
-        v_xq.append(quant(T.xq[:, 128 * k:128 * k + 128], T.xsc[:, 128 * k:128 * k + 128], T.xs[:, 512 * k:512 * k + 512]))
+    def unpack(name, after, b, codes, scales, lo, cnt):
+        op(name, after, lambda q: g.tensor.matmul_mx(T.pun[:, 512 * b:512 * b + cnt], T.eq[:, 128 * b:128 * b + 128],
+                                                     T.es[:, 128 * b:128 * b + 128], T[codes][:, lo:lo + cnt],
+                                                     T[scales][:, lo:lo + cnt], True, True))
 
-    def unpack(b, codes, scales, lo):
-        c = 128 * b
-        return did("ten", g.tensor.matmul_mx(T.pun[:, 512 * b:512 * b + 128], T.eq[:, c:c + 128], T.es[:, c:c + 128],
-                                             T[codes][:, lo:lo + 128], T[scales][:, lo:lo + 128], True, True))
-
-    def unpack_x(k, b, after):
-        need("ten", "vec", max(v_eq, v_xq[k]))
-        if after:
-            need("ten", ENG[b], after)
-        return unpack(b, "xq", "xsc", 128 * k)
-
-    def cast(k, b, t):
-        need(ENG[b], "ten", t)
-        c = TX * b + 128 * k
-        return copy(ENG[b], T.db[:, c:c + 128], T.pun[:, 512 * b:512 * b + 128])
-
-    def gather_near(q, t):
-        need(q, "vec", v_o4)
-        need(q, "ldx0", 16)
-        need(q, "ldx1", 16)
-        return copy(q, T.hn[:, t:512:4], T.xs[:, 0:4 * TX].indirect(T.off4[:, 8 * t:8 * t + 8]))
-
-    def gather(q, buf, c, k, t):
-        need(q, ENG[t], cx[t])
-        return copy(q, T[buf][:, t:64 * k:4], T.db[:, TX * t:TX * t + TX].indirect(T.offs[:, c:c + k]))
-
-    quant_x(0)
-    tx = [unpack_x(0, b, None) for b in range(4)]
-    need("vec", "vec", v_pl)
-    ts("pu1", "pl", 15, A.bitwise_and)
-    ts("pn", "pl", 0.0, A.is_lt)
-    v_pl = ts("pv", "pl", 4, A.arith_shift_right)
-    c0 = [cast(0, b, tx[b]) for b in (0, 1)]
-    quant_x(1)
-
-    gather_near("vec", 0)
-    gather_near("act", 1)
-    vv = gather_near("vec", 2)
-    aa = gather_near("act", 3)
-    need("vec", "vec", vv)
-    need("vec", "act", aa)
-    q0 = 96 * (1 - pos)
-    v_qn = quant(T.cq[:, q0:q0 + 128], T.cs[:, q0:q0 + 128], T.hn[:])
-    need("gps", "vec", v_qn)
-    rid, pid, _ = topo.addr(T.cores[mate])
-    sent = slice(128, 224) if pos == 0 else slice(0, 96)
-    g.remote_dma(T.cq[:, sent].bitcast(dt.uint8), T.cq[:, sent].bitcast(dt.uint8), T.sem.an, T.sem.sent, pid, rid, mask(mate, 0, 1))
-    g.remote_dma(T.cs[:, sent], T.cs[:, sent], T.sem.an, T.sem.sent, pid, rid, mask(mate, 0, 1))
-
-    need("vec", "vec", v_pl)
-    need("vec", "gps", p_all)
-    v_pw = ts("pw", "pu1", 64.0, A.mult)
-    v_pm = tt("pm", T.pn[:], T.dump[:], A.mult)
-    c0 += [cast(0, b, tx[b]) for b in (2, 3)]
-    need("vec", "vec", v_pm)
-    v_pp = tt("pp", T.pw[:], T.pv[:], A.add)
-    tx = [unpack_x(1, b, c0[b]) for b in range(4)]
-    cx = [cast(1, b, tx[b]) for b in (0, 1)]
-    c_far = LC * far[0]
-    need("vec", "vec", v_pp)
-    v_pf = tt("pf", T.pp[:], T.pm[:], A.max)
-    vv = gather("vec", "hf", c_far, 12, 0)
-    gather("act", "hf", c_far, 12, 1)
-    cx += [cast(1, b, tx[b]) for b in (2, 3)]
-    need("vec", "vec", v_pf)
-    v_op = did("vec", g.vector.tensor_copy(T.offp[:], T.pf[:]))
-    need("vec", "vec", v_op)
-    need("vec", "act", a_win)
-    v_in = did("vec", g.vector.tensor_copy(T.win[:, 0:WW].indirect(T.offp[:, 0:LC]), T.vals[:]))
-    need("syn", "vec", v_in)
-    for h in range(N):
-        for q in range(2):
-            g.sync.dma_start(T.inv4[16 * q:16 * q + 16, 64 * h:64 * h + 64], T.win[16 * h:16 * h + 1, 0:TC]).then_inc(T.sem.inv, 16)
-    gather("act", "hf", c_far, 12, 3)
-    aa = gather("act", "hf", c_far, 12, 2)
-    need("vec", "vec", vv)
-    need("vec", "act", aa)
-    v_qf = quant(T.sq[:], T.ss[:], T.hf[:])
-    need("gps", "vec", v_qf)
-    land = slice(CAPP * pos, CAPP * pos + CAPP)
-    for codes in (True, False):
-        tr = []
-        for k in range(2):
-            here = slice(CAPP * k, CAPP * k + CAPP)
-            if codes:
-                a, b = T.sq[:, here].bitcast(dt.uint8), T.lq[:, land].bitcast(dt.uint8)
-            else:
-                a, b = T.ss[:, here], T.ls[:, land]
-            tr.append(RemoteDMATransfer(dst_ids=[dst(far[k])], dma_engine_mask=mask(far[k], k, 2), remote_sem=T.sem.af, src=a, dst=b))
-        g.remote_dma_fused(tr, local_sem=T.sem.sent)
-
-    def times(bank, codes, scales, a, b):
-        return did("ten", g.tensor.matmul_mx(T.pro[:, 512 * bank:512 * bank + b - a], T.wq[:], T.ws[:], T[codes][:, a:b], T[scales][:, a:b], True, True))
-
-    KC = ((0, 512, 0, "act"), (512, 768, 1, "act"), (768, 1024, 3, "vec"))
-
-    def quant_kc(k):
-        a, b = KC[k][:2]
-        need("vec", "ldk%d" % (a // 512), 16)
-        return quant(T.kq[:, a:b], T.ks[:, a:b], T.kcs[:, 4 * a:4 * b])
-
-    def times_kc(k, v):
-        a, b, bank, q = KC[k]
-        need("ten", "vec", v)
-        return times(bank, "kq", "ks", a, b)
-
-    def take_kc(k, t):
-        a, b, bank, q = KC[k]
-        need(q, "ten", t)
-        return copy(q, T.yb[:, a:b], T.pro[:, 512 * bank:512 * bank + b - a])
-
-    def take(r, cnt, bank, col, t):
-        need("act", "ten", t)
-        c = TC + CAPP * r
-        return copy("act", T.yb[:, c:c + cnt], T.pro[:, 512 * bank + col:512 * bank + col + cnt])
-
-    for t in range(4):
-        aa = gather("act", "ho", c_own, 8, t)
-    need("vec", "ldw", 16)
-    v_wq = quant(T.wq[:], T.ws[:], T.qws[:])
-    v_k = [quant_kc(0)]
-    need("vec", "act", aa)
-    v_oq = quant(T.oq[:], T.osc[:], T.ho[:])
-    v_k += [quant_kc(1), quant_kc(2)]
-    need("ten", "vec", v_wq)
-    t_k = [times_kc(0, v_k[0])]
-    need("ten", "vec", v_oq)
-    t_o = times(2, "oq", "osc", 0, 128)
-    a_k = take_kc(0, t_k[0])
-    a_o = take(rank, CAPP, 2, 32 * pos, t_o)
-
-    need("ten", "an", 32)
     for b in range(4):
-        need("ten", ENG[b], cx[b])
-    p0 = 0 if pos == 0 else 96
-    tn = [unpack(b, "cq", "cs", p0) for b in range(4)]
+        unpack("u%d" % b, "xq0 xq1 eq%d" % b, b, "xq", "xsc", 0, TX)
+        copy("cast%d" % b, "u%d" % b, T.db[:, TX * b:TX * b + TX], T.pun[:, 512 * b:512 * b + TX])
+        for w, r, m in (("f", far[0], 2), ("o", rank, 1)):
+            copy("g%s%d" % (w, b), "cast%d of0 of1" % b, T["h" + w][:, b:384 * m:4],
+                 T.db[:, TX * b:TX * b + TX].indirect(T.offs[:, LC * r:LC * r + LC * m]))
+    quant("qf", "gf0 gf1 gf2 gf3", "fq", "fs", 0, 192, "hf", 0)
+    quant("oq", "zo go0 go1 go2 go3", "oq", "osc", 0, 128, "ho", 0)
+
+    def send_far(q):
+        land = slice(CAPP * pos, CAPP * pos + CAPP)
+        for codes in (True, False):
+            tr = []
+            for k in range(2):
+                here = slice(CAPP * k, CAPP * k + CAPP)
+                if codes:
+                    a, b = T.fq[:, here].bitcast(dt.uint8), T.lq[:, land].bitcast(dt.uint8)
+                else:
+                    a, b = T.fs[:, here], T.ls[:, land]
+                rid, pid, _ = topo.addr(T.cores[far[k]])
+                tr.append(RemoteDMATransfer(dst_ids=[DstId(rid=rid, pnc=pid)], dma_engine_mask=mask(far[k], k, 2),
+                                            remote_sem=T.sem.af, src=a, dst=b))
+            g.remote_dma_fused(tr, local_sem=T.sem.sent)
+
+    op("sf", "qf", send_far)
+
     for b in range(4):
-        need("act", "ten", tn[b])
-        aa = copy("act", T.dn[:, b:512:4], T.pun[:, 512 * b:512 * b + 128])
-    t_k += [times_kc(1, v_k[1]), times_kc(2, v_k[2])]
-    take_kc(1, t_k[1])
-    need("vec", "inv", 128)
-    v = tt("mx1", T.inv4[:, 0:128], T.inv4[:, 128:256], A.max)
-    need("vec", "vec", v)
-    v = tt("mx2", T.mx1[:, 0:64], T.mx1[:, 64:128], A.max)
-    need("vec", "act", aa)
-    v_nq = quant(T.nq[:], T.nsc[:], T.dn[:])
-    need("vec", "vec", v)
-    v = tt("mx3", T.mx2[:], T.ident[:], A.max)
-    take_kc(2, t_k[2])
-    need("vec", "vec", v)
-    for q in (0, 32, 64, 96):
-        v_oy = did("vec", g.vector.tensor_copy(T.offy[q:q + 32, :], T.mx3[:]))
-    need("ten", "vec", v_nq)
-    need("ten", "act", a_o)
-    t_n = times(2, "nq", "nsc", 0, 128)
-    take(mate, CAPP, 2, 32 * pos, t_n)
+        unpack("r%d" % b, "@an qn eq%d cast%d" % (b, b), b, "nq", "ns", 96 * pos, 128)
+        c = 512 * b + 32 * pos
+        copy("dc%d" % b, "r%d" % b, T.dn[:, b:384:4], T.pun[:, c:c + CAPP])
+    quant("dq", "zd dc0 dc1 dc2 dc3", "dq", "dsc", 0, 128, "dn", 0)
 
-    need("ten", "af", 32)
-    need("ten", "act", a_k)
-    t_f = times(0, "lq", "ls", 0, 192)
-    a_y = take(far[0], 2 * CAPP, 0, 0, t_f)
+    quant("wq", "@ldw", "wq", "ws", 0, 128, "qws", 0)
 
-    for q in ("vec", "act"):
-        need(q, "vec", v_oy)
-        need(q, "act", a_y)
-    cut = (0, 12, 24, 44, 64)
-    for k in range(2):
-        for q, c in (("vec", 2 * k), ("act", 2 * k + 1)):
-            lo, hi = cut[c], cut[c + 1]
-            copy(q, T.yo[:, 16 * lo:16 * hi], T.yb[:, 0:SRC].indirect(T.offy[:, lo:hi]))
-        need("syn", "vec", n["vec"])
-        need("syn", "act", n["act"])
-        lo, hi = 16 * cut[2 * k], 16 * cut[2 * k + 2]
-        g.sync.dma_start(T.y[:, lo:hi], T.yo[:, lo:hi]).then_inc(T.sem["st%d" % k], 16)
+    def times(name, after, buf, bank, codes, scales, a, b, to, cnt):
+        out = T[buf][:, 512 * bank:512 * bank + b - a]
+        op(name, "wq " + after, lambda q: g.tensor.matmul_mx(out, T.wq[:], T.ws[:], T[codes][:, a:b], T[scales][:, a:b], True, True))
+        copy("c" + name, name, T.yb[:, to:to + cnt], T[buf][:, 512 * bank:512 * bank + cnt])
+
+    for k, (a, b) in enumerate(KC):
+        quant("kq%d" % k, "@ldk%d" % (a // 512), "kq", "ks", a, b, "kcs", 4 * a)
+        times("k%d" % k, "kq%d" % k, "pro", k, "kq", "ks", a, b, a, b - a)
+    times("o", "oq", "pro", 3, "oq", "osc", 0, 128, TC + CAPP * rank, CAPP)
+    times("n", "dq dc1", "pun", 1, "dq", "dsc", 0, 128, TC + CAPP * mate, CAPP)
+    times("f", "@af dc0", "pun", 0, "lq", "ls", 0, 192, TC + CAPP * far[0], 2 * CAPP)
+
+    ready = "oy0 oy1 oy2 oy3 cf co cn ck0 ck1 ck2"
+    for k in range(PIECES):
+        for w, c in (("v", 2 * k), ("a", 2 * k + 1)):
+            lo, hi = CUT[c], CUT[c + 1]
+            copy("y%s%d" % (w, k), ready, T.yo[:, 16 * lo:16 * hi], T.yb[:, 0:SRC].indirect(T.offy[:, lo:hi]))
+        op("st%d" % k, "yv%d ya%d" % (k, k), lambda q, k=k, lo=16 * CUT[2 * k], hi=16 * CUT[2 * k + 2]:
+           g.sync.dma_start(T.y[:, lo:hi], T.yo[:, lo:hi]).then_inc(T.sem["st%d" % k], 16))
+
+    todo = {q: ORDER[q].split() for q in ORDER}
+    done, n, seen = {}, {q: 0 for q in ORDER}, {}
+
+    def need(q, key, val):
+        if seen.get((q, key), 0) < val:
+            Q[q].wait_ge(T.sem[key], val)
+            seen[(q, key)] = val
+
+    moved = True
+    while moved:
+        moved = False
+        for q in todo:
+            while todo[q]:
+                after, call = ops[todo[q][0]]
+                if any(a[0] != "@" and a not in done for a in after):
+                    break
+                for a in after:
+                    key, val = (a[1:], count[a[1:]]) if a[0] == "@" else done[a]
+                    if key in n:
+                        val = max(done[a][1] for a in after if a in done and done[a][0] == key)
+                    need(q, key, val)
+                name, moved = todo[q].pop(0), True
+                made = call(q)
+                if q != "syn" and name not in ("sn", "sf"):
+                    n[q] += 1
+                    made.then_inc(T.sem[q], 1)
+                    done[name] = (q, n[q])
+    assert not any(todo.values())
 
     need("gps", "sent", 64)
     for q in ("vec", "act", "ten", "gps"):
         need("gps", q, n[q])
-    for k in range(2):
+    for k in range(PIECES):
         g.sync.wait_ge(T.sem["st%d" % k], 16)

from concourse.bass import DstId, RemoteDMATransfer
from concourse.mybir import dt, AluOpType, ActivationFunctionType

TC, TX, CAPP, N = 1024, 256, 96, 4
LC = CAPP // 16
WW = 1232
SRC = TC + N * CAPP
BF, F32, I32, U16, U8, C8 = "bfloat16", "float32", "int32", "uint16", "uint8", "float8_e4m3fn_x4"

SCRATCH = {
    "sl": ("sbuf", [64, N * LC], I32),
    "offs": ("sbuf", [128, N * LC], U16),
    "off4": ("sbuf", [128, 4 * LC], U16),
    "xs": ("sbuf", [128, 4 * TX], BF),
    "kcs": ("sbuf", [128, 4 * TC], BF),
    "qws": ("sbuf", [128, 512], BF),
    "xq": ("sbuf", [128, TX], C8), "xsc": ("sbuf", [128, TX], U8),
    "db": ("sbuf", [128, 4 * TX], BF),
    "hn": ("sbuf", [128, 512], BF), "hf": ("sbuf", [128, 768], BF), "ho": ("sbuf", [128, 512], BF),
    "nq": ("sbuf", [128, 224], C8), "ns": ("sbuf", [128, 224], U8),
    "fq": ("sbuf", [128, 192], C8), "fs": ("sbuf", [128, 192], U8),
    "lq": ("sbuf", [128, 192], C8), "ls": ("sbuf", [128, 192], U8),
    "oq": ("sbuf", [128, 128], C8), "osc": ("sbuf", [128, 128], U8),
    "dn": ("sbuf", [128, 512], BF),
    "dq": ("sbuf", [128, 128], C8), "dsc": ("sbuf", [128, 128], U8),
    "ones": ("sbuf", [128, 128], BF),
    "ed": ("sbuf", [128, 516], BF),
    "eq": ("sbuf", [128, 512], C8), "es": ("sbuf", [128, 512], U8),
    "wq": ("sbuf", [128, 128], C8), "ws": ("sbuf", [128, 128], U8),
    "kq": ("sbuf", [128, TC], C8), "ks": ("sbuf", [128, TC], U8),
    "win": ("sbuf", [128, WW], F32),
    "vals": ("sbuf", [128, CAPP], F32),
    "dump": ("sbuf", [128, LC], I32),
    "pl": ("sbuf", [128, LC], I32), "pu": ("sbuf", [128, LC], I32), "pv": ("sbuf", [128, LC], I32),
    "pw": ("sbuf", [128, LC], I32), "pp": ("sbuf", [128, LC], I32), "pf": ("sbuf", [128, LC], I32),
    "offp": ("sbuf", [128, LC], U16),
    "pa": ("sbuf", [32, 1], F32), "pc": ("sbuf", [32, 1], F32),
    "inv4": ("sbuf", [32, 256], F32), "mx1": ("sbuf", [32, 128], F32), "mx2": ("sbuf", [32, 64], F32),
    "offy": ("sbuf", [128, 64], U16),
    "yb": ("sbuf", [128, SRC], F32),
    "yo": ("sbuf", [128, TC], F32),
    "pun": ("psum", [128, 2048], F32),
    "pro": ("psum", [128, 2048], F32),
}
SEMAPHORES = ["ldl", "ldx0", "ldx1", "ldp", "ldw", "ldk0", "ldk1", "vec", "act", "ten", "gps", "inv", "af", "an", "sent",
              "st0", "st1", "st2"]
CUT = (0, 8, 16, 28, 40, 52, 64)
PIECES = len(CUT) // 2
KC = ((0, 512), (512, 768), (768, 1024))
ORDER = {
    "gps": "win0 aff dump pl vals sn pa sf pc",
    "act": "win2 win4 win8 zn gn3 gn1 gn0 cast1 gf1 cast2 cast3 gf3 zd zo go2 go1 go0 go3 ck0 dc1 dc3 dc0 co ck1 ck2 cn "
           "ya0 ya1 ya2",
    "vec": "ed ones eq0 eq3 of0 eq1 of1 pv o42 o43 o41 o40 xq1 xq0 gn2 pu eq2 pw qn pp cast0 pf wq op gf0 sc gf2 qf "
           "kq0 kq2 oq kq1 mx1 mx2 oy3 oy1 dc2 oy0 dq oy2 cf yv0 yv1 yv2",
    "ten": "u1 u0 u2 u3 k0 o r3 r1 r2 r0 k1 k2 f n",
    "syn": "inv st0 st1 st2",
}


def rank_program(g, core, T, topo):
    rank = T.rank_of(core)
    if rank is None:
        return
    A, COPY, IDENT = AluOpType, ActivationFunctionType.Copy, ActivationFunctionType.Identity
    V, S = g.vector, g.scalar
    Q = {"vec": V, "act": S, "ten": g.tensor, "gps": g, "syn": g.sync}

    die = [topo.die(c) for c in T.cores]
    near = [r for r in range(N) if die[r] == die[rank]]
    far = [r for r in range(N) if die[r] != die[rank]]
    pos = near.index(rank)
    mate = near[1 - pos]

    def mask(r, k, step):
        return sum(1 << e for e in topo.engines(core, T.cores[r])[k::step])

    for h in range(4):
        q = g.sync if h % 2 else g.scalar
        q.dma_start(T.sl[16 * h:16 * h + 16, :], T.snd[:]).then_inc(T.sem.ldl, 16)
    for h in range(N):
        q = g.sync if h % 2 else g.scalar
        q.dma_start(T.pl[16 * h:16 * h + 16, :], T.plc[:, LC * h:LC * h + LC]).then_inc(T.sem.ldp, 16)
    g.sync.dma_start(T.xs[:, 0:512], T.x[:, 0:512]).then_inc(T.sem.ldx0, 16)
    g.scalar.dma_start(T.xs[:, 512:1024], T.x[:, 512:1024]).then_inc(T.sem.ldx1, 16)
    g.scalar.dma_start(T.qws[:], T.qw[:]).then_inc(T.sem.ldw, 16)
    for k in range(2):
        g.sync.dma_start(T.kcs[:, 2048 * k:2048 * k + 2048], T.kc[:, 2048 * k:2048 * k + 2048]).then_inc(T.sem["ldk%d" % k], 16)
    count = {"ldl": 64, "ldp": 64, "ldx0": 16, "ldx1": 16, "ldw": 16, "ldk0": 16, "ldk1": 16, "an": 32, "af": 32, "inv": 64}

    ops = {}

    def op(name, after, call):
        ops[name] = (after.split(), call)

    def quant(name, after, codes, scales, lo, hi, tile, start):
        op(name, after, lambda q: V.quantize_mx(T[codes][:, lo:hi], T[scales][:, lo:hi], T[tile][:, start:start + 4 * (hi - lo)]))

    def copy(name, after, out, in_):
        op(name, after, lambda q: V.tensor_copy(out, in_) if q == "vec" else S.activation(out, in_, COPY))

    def ts(name, after, o, a, c, f):
        op(name, after, lambda q: V.tensor_scalar(T[o][:], T[a][:], c, None, f))

    def tt(name, after, o, a, b, f):
        op(name, after, lambda q: V.tensor_tensor(T[o][:], a, b, f))

    op("ones", "", lambda q: V.memset(T.ones[:], 1.0))
    op("ed", "", lambda q: V.memset(T.ed[:], 0.0))
    op("aff", "ones ed", lambda q: g.affine_select(T.ed[:, 4:516:4], T.ones[:], [[-1, 128]], A.is_equal, 0.0, 0, 1))
    for b in range(4):
        quant("eq%d" % b, "aff", "eq", "es", 128 * b, 128 * b + 128, "ed", 4 - b)
    zn = 384 * pos
    for name, o in (("zn", T.hn[:, zn:zn + 128]), ("zo", T.ho[:, 384:512]), ("zd", T.dn[:, 384:512])):
        op(name, "ones", lambda q, o=o: S.activation(o, T.ones[:], COPY, 0.0, 0.0))

    imp = {"allow_small_or_imprecise_dtypes": True}
    op("win0", "", lambda q: g.iota(T.win[:, 0:128], [[1, 2], [16, 64]], -3 * CAPP, LC, **imp))
    for k, b in ((2, 0), (4, 2), (8, 4)):
        op("win%d" % k, "win0 win%d" % b, lambda q, k=k: S.activation(T.win[:, 64 * k:128 * k], T.win[:, 0:64 * k], IDENT, float(k)))
    op("dump", "", lambda q: g.iota(T.dump[:], [[16, LC]], TC, 1))
    op("pl", "dump", lambda q: g.iota(T.pl[64:128, :], [[16, LC]], 0, 1))
    op("vals", "pl", lambda q: g.iota(T.vals[:], [[1, CAPP]], TC, LC, **imp))
    op("pa", "vals", lambda q: g.iota(T.pa[:], [[0, 1]], LC, 0, **imp))
    op("pc", "pa", lambda q: g.affine_select(T.pc[:], T.pa[:], [[0, 1]], A.is_ge, 0.0, -16, 1))
    ts("pu", "@ldp pl", "pu", "pl", 15, A.bitwise_and)
    ts("pv", "@ldp pl", "pv", "pl", 4, A.logical_shift_right)
    ts("pw", "pu", "pw", "pu", 64.0, A.mult)
    tt("pp", "pw pv", "pp", T.pw[:], T.pv[:], A.add)
    tt("pf", "pp dump", "pf", T.pp[:], T.dump[:], A.min)
    copy("op", "pf", T.offp[:], T.pf[:])
    copy("sc", "op vals win0 win8", T.win[:, 0:WW].indirect(T.offp[:, 0:LC]), T.vals[:])

    def lay_out(q):
        for h in range(N):
            g.sync.dma_start(T.inv4[:, 64 * h:64 * h + 64], T.win[16 * h:16 * h + 2, 0:TC]).then_inc(T.sem.inv, 16)

    op("inv", "sc", lay_out)
    tt("mx1", "@inv", "mx1", T.inv4[:, 0:128], T.inv4[:, 128:256], A.max)
    tt("mx2", "mx1", "mx2", T.mx1[:, 0:64], T.mx1[:, 64:128], A.max)
    for k in range(4):
        op("oy%d" % k, "mx2 pc", lambda q, k=k: V.tensor_scalar(T.offy[32 * k:32 * k + 32, :], T.mx2[:], T.pc[:], None, A.subtract))

    for k in range(2):
        copy("of%d" % k, "@ldl", T.offs[64 * k:64 * k + 64, :], T.sl[:])
        quant("xq%d" % k, "@ldx%d" % k, "xq", "xsc", 128 * k, 128 * k + 128, "xs", 512 * k)
    lo = 128 * (1 - pos)
    for b in range(4):
        op("o4%d" % b, "of0 of1", lambda q, b=b: V.tensor_scalar(T.off4[:, LC * b:LC * b + LC], T.offs[:, LC * mate:LC * mate + LC],
                                                                 4.0, float(b), A.mult, A.add))
        copy("gn%d" % b, "o4%d @ldx0 @ldx1" % b, T.hn[:, lo + b:lo + 384:4], T.xs[:, 0:4 * TX].indirect(T.off4[:, LC * b:LC * b + LC]))
    tile = 96 * (1 - pos)
    quant("qn", "zn gn0 gn1 gn2 gn3", "nq", "ns", tile, tile + 128, "hn", 0)

    def send_near(q):
        rid, pid, _ = topo.addr(T.cores[mate])
        here = slice(128, 224) if pos == 0 else slice(0, 96)
        g.remote_dma(T.nq[:, here].bitcast(dt.uint8), T.nq[:, here].bitcast(dt.uint8), T.sem.an, T.sem.sent, pid, rid, mask(mate, 0, 1))
        g.remote_dma(T.ns[:, here], T.ns[:, here], T.sem.an, T.sem.sent, pid, rid, mask(mate, 0, 1))

    op("sn", "qn", send_near)

    def unpack(name, after, b, codes, scales, lo, cnt):
        op(name, after, lambda q: g.tensor.matmul_mx(T.pun[:, 512 * b:512 * b + cnt], T.eq[:, 128 * b:128 * b + 128],
                                                     T.es[:, 128 * b:128 * b + 128], T[codes][:, lo:lo + cnt],
                                                     T[scales][:, lo:lo + cnt], True, True))

    for b in range(4):
        unpack("u%d" % b, "xq0 xq1 eq%d" % b, b, "xq", "xsc", 0, TX)
        copy("cast%d" % b, "u%d" % b, T.db[:, TX * b:TX * b + TX], T.pun[:, 512 * b:512 * b + TX])
        for w, r, m in (("f", far[0], 2), ("o", rank, 1)):
            copy("g%s%d" % (w, b), "cast%d of0 of1" % b, T["h" + w][:, b:384 * m:4],
                 T.db[:, TX * b:TX * b + TX].indirect(T.offs[:, LC * r:LC * r + LC * m]))
    quant("qf", "gf0 gf1 gf2 gf3", "fq", "fs", 0, 192, "hf", 0)
    quant("oq", "zo go0 go1 go2 go3", "oq", "osc", 0, 128, "ho", 0)

    def send_far(q):
        land = slice(CAPP * pos, CAPP * pos + CAPP)
        for codes in (True, False):
            tr = []
            for k in range(2):
                here = slice(CAPP * k, CAPP * k + CAPP)
                if codes:
                    a, b = T.fq[:, here].bitcast(dt.uint8), T.lq[:, land].bitcast(dt.uint8)
                else:
                    a, b = T.fs[:, here], T.ls[:, land]
                rid, pid, _ = topo.addr(T.cores[far[k]])
                tr.append(RemoteDMATransfer(dst_ids=[DstId(rid=rid, pnc=pid)], dma_engine_mask=mask(far[k], k, 2),
                                            remote_sem=T.sem.af, src=a, dst=b))
            g.remote_dma_fused(tr, local_sem=T.sem.sent)

    op("sf", "qf", send_far)

    for b in range(4):
        unpack("r%d" % b, "@an qn eq%d cast%d" % (b, b), b, "nq", "ns", 96 * pos, 128)
        c = 512 * b + 32 * pos
        copy("dc%d" % b, "r%d" % b, T.dn[:, b:384:4], T.pun[:, c:c + CAPP])
    quant("dq", "zd dc0 dc1 dc2 dc3", "dq", "dsc", 0, 128, "dn", 0)

    quant("wq", "@ldw", "wq", "ws", 0, 128, "qws", 0)

    def times(name, after, buf, bank, codes, scales, a, b, to, cnt):
        out = T[buf][:, 512 * bank:512 * bank + b - a]
        op(name, "wq " + after, lambda q: g.tensor.matmul_mx(out, T.wq[:], T.ws[:], T[codes][:, a:b], T[scales][:, a:b], True, True))
        copy("c" + name, name, T.yb[:, to:to + cnt], T[buf][:, 512 * bank:512 * bank + cnt])

    for k, (a, b) in enumerate(KC):
        quant("kq%d" % k, "@ldk%d" % (a // 512), "kq", "ks", a, b, "kcs", 4 * a)
        times("k%d" % k, "kq%d" % k, "pro", k, "kq", "ks", a, b, a, b - a)
    times("o", "oq", "pro", 3, "oq", "osc", 0, 128, TC + CAPP * rank, CAPP)
    times("n", "dq dc1", "pun", 1, "dq", "dsc", 0, 128, TC + CAPP * mate, CAPP)
    times("f", "@af dc0", "pun", 0, "lq", "ls", 0, 192, TC + CAPP * far[0], 2 * CAPP)

    ready = "oy0 oy1 oy2 oy3 cf co cn ck0 ck1 ck2"
    for k in range(PIECES):
        for w, c in (("v", 2 * k), ("a", 2 * k + 1)):
            lo, hi = CUT[c], CUT[c + 1]
            copy("y%s%d" % (w, k), ready, T.yo[:, 16 * lo:16 * hi], T.yb[:, 0:SRC].indirect(T.offy[:, lo:hi]))
        op("st%d" % k, "yv%d ya%d" % (k, k), lambda q, k=k, lo=16 * CUT[2 * k], hi=16 * CUT[2 * k + 2]:
           g.sync.dma_start(T.y[:, lo:hi], T.yo[:, lo:hi]).then_inc(T.sem["st%d" % k], 16))

    todo = {q: ORDER[q].split() for q in ORDER}
    done, n, seen = {}, {q: 0 for q in ORDER}, {}

    def need(q, key, val):
        if seen.get((q, key), 0) < val:
            Q[q].wait_ge(T.sem[key], val)
            seen[(q, key)] = val

    moved = True
    while moved:
        moved = False
        for q in todo:
            while todo[q]:
                after, call = ops[todo[q][0]]
                if any(a[0] != "@" and a not in done for a in after):
                    break
                for a in after:
                    key, val = (a[1:], count[a[1:]]) if a[0] == "@" else done[a]
                    if key in n:
                        val = max(done[a][1] for a in after if a in done and done[a][0] == key)
                    need(q, key, val)
                name, moved = todo[q].pop(0), True
                made = call(q)
                if q != "syn" and name not in ("sn", "sf"):
                    n[q] += 1
                    made.then_inc(T.sem[q], 1)
                    done[name] = (q, n[q])
    assert not any(todo.values())

    need("gps", "sent", 64)
    for q in ("vec", "act", "ten", "gps"):
        need("gps", q, n[q])
    for k in range(PIECES):
        g.sync.wait_ge(T.sem["st%d" % k], 16)
